import numpy as np
import ml_dtypes


def mxq(x, axis, fmt="e4m3"):
    dtype, down = {"e4m3": (ml_dtypes.float8_e4m3fn, 7), "e5m2": (ml_dtypes.float8_e5m2, 14)}[fmt]
    v = np.moveaxis(np.asarray(x, np.float32).astype(ml_dtypes.bfloat16).astype(np.float64), axis, -1)
    blocks = v.reshape(v.shape[:-1] + (-1, 32))
    amax = np.abs(blocks).max(-1, keepdims=True)
    byte = np.maximum(np.where(amax > 0, np.frexp(amax)[1] - 1 + 127, 0) - down, 1)
    scale = np.exp2(byte - 127.0)
    codes = (blocks / scale).astype(np.float32).astype(dtype).astype(np.float64)
    return np.moveaxis((codes * scale).reshape(v.shape), -1, axis)


WIDE = False


def mx_kscale(k):
    if not WIDE:
        return np.ones(k)
    levels = np.array([10, -10, 5, -5, 0])
    if k % 512:
        return np.exp2(np.random.permutation(np.resize(levels, k // 32))).repeat(32)
    a = np.empty((k // 512, 16))
    for p in range(k // 512):
        a[p, :8] = np.random.permutation(np.resize(levels, 8))
        for g in range(8):
            far = levels[np.abs(levels - a[p, g]) >= 10]
            a[p, g + 8] = far[np.random.randint(len(far))]
    return np.exp2(a.ravel()).repeat(32)


def f64(x):
    return np.asarray(x).astype(np.float64)


def striped(idx):
    return np.tile(idx.reshape(-1, 16).T, (8, 1)).astype(np.uint16)


def unstriped(offs):
    return offs[:16].T.reshape(-1).astype(np.int64)


E2M1 = np.array([0.0, 0.5, 1.0, 1.5, 2.0, 3.0, 4.0, 6.0, -0.0, -0.5, -1.0, -1.5, -2.0, -3.0, -4.0, -6.0])


def pack_weight(w, fmt):
    k, n = w.shape
    w = f64(np.asarray(w, np.float32).astype(ml_dtypes.bfloat16)).reshape(k // 32, 32, n)
    amax = np.abs(w).max(1)
    if fmt == "e4m3":
        byte = np.frexp(amax)[1] - 1 + 127 - 7
    else:
        mant, ex = np.frexp(amax / 6.0)
        byte = np.where(mant > 0.5, ex, ex - 1) + 127
    byte = np.clip(np.where(amax > 0, byte, 1), 1, 254)
    scaled = (w * np.exp2(127.0 - byte)[:, None, :]).reshape(k, n).astype(np.float32)
    by_word = np.ascontiguousarray(scaled.reshape(k // 512, 128, 4, n).transpose(0, 1, 3, 2))
    if fmt == "e4m3":
        words = by_word.astype(ml_dtypes.float8_e4m3fn).view(np.uint8)
    else:
        c = by_word.astype(ml_dtypes.float4_e2m1fn).view(np.uint8) & 0xF
        words = (c[..., 0::2] | (c[..., 1::2] << 4)).reshape(k // 512, 128, 2 * n)
    return np.ascontiguousarray(words), np.ascontiguousarray(byte.astype(np.uint8).reshape(k // 512, 16, n))


def unpack_weight(words, scales, fmt):
    g, _, n = scales.shape
    words = np.ascontiguousarray(words).reshape(g, 128, n, -1)
    if fmt == "e4m3":
        vals = words.view(ml_dtypes.float8_e4m3fn).astype(np.float64)
    else:
        nib = np.empty((g, 128, n, 4), np.uint8)
        nib[..., 0::2] = words & 0xF
        nib[..., 1::2] = words >> 4
        vals = E2M1[nib]
    vals = vals * np.repeat(np.exp2(scales.astype(np.float64) - 127.0), 8, axis=1)[..., None]
    return vals.transpose(0, 1, 3, 2).reshape(g * 512, n)


def gelu(v):
    return 0.5 * v * (1.0 + np.tanh(np.sqrt(2.0 / np.pi) * (v + 0.044715 * v**3)))


K, T, E, C, N = 1536, 640, 20, 128, 128
TOP = 4
K8 = 512


def by_expert(wq, xq):
    return np.concatenate([wq[e].T @ xq[:, e * C:(e + 1) * C] for e in range(E)], axis=1)


def setup_inputs():
    n = np.random.standard_normal
    s = mx_kscale(K)[:, None]
    deal = np.repeat(np.arange(E), C).reshape(TOP, T)[:, np.random.permutation(T)]
    deal = np.take_along_axis(deal, np.argsort(np.random.rand(TOP, T), axis=0), axis=0)
    for _ in range(8):
        s_, t_ = np.random.permutation(T).reshape(2, -1); r = np.random.randint(TOP, size=T // 2); x, y = deal[r, s_].copy(), deal[r, t_].copy()
        ok = ~((deal[:, s_] == y).any(0) | (deal[:, t_] == x).any(0)); deal[r[ok], s_[ok]] = y[ok]; deal[r[ok], t_[ok]] = x[ok]
    order = np.lexsort((np.random.rand(TOP * T), deal.reshape(-1)))
    slot_token = order % T; pos = np.empty(TOP * T, np.int64); pos[order] = np.arange(TOP * T); pos = pos.reshape(TOP, T)
    g = np.random.uniform(0.5, 1.5, (TOP, T)); g = g / g.sum(0)
    w = n((E, K, N)) / np.sqrt(K) / s[None]
    w8 = [pack_weight(m[:K8], "e4m3") for m in w]
    w4 = [pack_weight(m[K8:], "e2m1") for m in w]
    return {
        "xT": (n((K, T)) * s).astype(np.float32),
        "w8_words": np.stack([m[0] for m in w8]),
        "w8_scales": np.stack([m[1] for m in w8]),
        "w4_words": np.stack([m[0] for m in w4]),
        "w4_scales": np.stack([m[1] for m in w4]),
        "b": (0.3 * n((N, E))).astype(np.float32),
        "gate": np.stack([np.tile(r, (N, 1)) for r in g]).astype(np.float32),
        "offs": striped(slot_token),
        "pos1": striped(pos[0]),
        "pos2": striped(pos[1]),
        "pos3": striped(pos[2]),
        "pos4": striped(pos[3]),
    }


def reference(xT, w8_words, w8_scales, w4_words, w4_scales, b, gate, offs, pos1, pos2, pos3, pos4):
    idx = unstriped(offs)
    w = np.stack([np.concatenate([unpack_weight(w8_words[e], w8_scales[e], "e4m3"), unpack_weight(w4_words[e], w4_scales[e], "e2m1")]) for e in range(E)])
    xq = mxq(f64(xT)[:, idx], 0, "e4m3")
    y = by_expert(w, xq)
    y = gelu(y + np.repeat(f64(b), C, axis=1))
    return sum(f64(gate[r]) * y[:, unstriped(p)] for r, p in enumerate((pos1, pos2, pos3, pos4)))

@@ -1,0 +1,203 @@
+from contextlib import ExitStack
+
+import concourse.mybir as mybir
+
+F32 = mybir.dt.float32
+BF16 = mybir.dt.bfloat16
+I32 = mybir.dt.int32
+U32 = mybir.dt.uint32
+U16 = mybir.dt.uint16
+U8 = mybir.dt.uint8
+FP8X4 = mybir.dt.float8_e4m3fn_x4
+FP4X4 = mybir.dt.float4_e2m1fn_x4
+MULT = mybir.AluOpType.mult
+ADD = mybir.AluOpType.add
+GELU = mybir.ActivationFunctionType.Gelu_apprx_tanh
+
+P = 128
+K, T, E, C, N, TOP = 1536, 640, 20, 128, 128, 4
+PASSES = 3
+S = E * C
+FLOPS = 2 * S * K * N
+
+WIN = 1728
+HALF = S // 2
+WIN2 = 704
+PLANE = (4, 0, 8)
+
+
+def tile_moe_tk_lin_gelu_kernel(
+    tc, xT, w8_words, w8_scales, w4_words, w4_scales, b, gate, offs, pos1, pos2, pos3, pos4, out
+):
+    nc = tc.nc
+    with ExitStack() as ctx:
+        lists = ctx.enter_context(tc.tile_pool(name="lists", bufs=1))
+        keep = ctx.enter_context(tc.tile_pool(name="keep", bufs=1))
+        psum = ctx.enter_context(tc.psum_pool(name="psum", bufs=6))
+
+        offs_sb = lists.tile([P, S // 16], U16, name="offs_sb")
+        pos_sb = [lists.tile([P, T // 16], U16, name=f"pos{r}_sb") for r in range(TOP)]
+
+        def x_rows(a):
+            return xT[512 * a : 512 * (a + 1), :].rearrange("(p j) t -> p j t", j=4)
+
+        x0a = keep.tile([P, 4, 512], F32, name="x0a")
+        x0b = keep.tile([P, 4, 128], F32, name="x0b")
+        x1 = keep.tile([P, 4, T], F32, name="x1")
+        x2 = keep.tile([P, 4, T], F32, name="x2")
+        nc.sync.dma_start(out=x0a[:], in_=x_rows(0)[:, :, 0:512])
+        nc.sync.dma_start(out=x0b[:], in_=x_rows(0)[:, :, 512:640])
+        nc.sync.dma_start(offs_sb[:], offs)
+        nc.sync.dma_start(out=x1[:], in_=x_rows(1))
+        nc.sync.dma_start(out=x2[:], in_=x_rows(2))
+
+        tiny = keep.tile([P, 8], F32, name="tiny")
+        tiny2 = keep.tile([P, 8], F32, name="tiny2")
+        nc.gpsimd.memset(tiny[:], 0.0)
+        nc.scalar.activation(out=tiny2[:], in_=tiny[:], func=GELU)
+        codes = [keep.tile([P, WIN if a < 1 else WIN2], I32, name=f"codes{a}", align_bytes=64) for a in range(PASSES)]
+        bytes_all = keep.tile([P, WIN], U8, name="bytes_all", align_bytes=64)
+        nc.gpsimd.memset(bytes_all[:], 0)
+        for a in range(PASSES):
+            nc.vector.memset(codes[a][:, T:], 0)
+        w8_s = keep.tile([P, E * N // 4], I32, name="w8_s", align_bytes=64)
+        w4_s = keep.tile([P, 2 * E * N // 4], I32, name="w4_s", align_bytes=64)
+        g_moved = keep.tile([P, S // 4], I32, name="g_moved", align_bytes=64)
+        nc.gpsimd.memset(w8_s[:], 0)
+        nc.gpsimd.memset(w4_s[:], 0)
+        nc.gpsimd.memset(g_moved[:], 0)
+
+        w8_src = w8_scales.bitcast(I32).rearrange("e a (q r) n -> q r (e a) n", r=4)
+        w4_src = w4_scales.bitcast(I32).rearrange("e a (q r) n -> q r (e a) n", r=4)
+        for q in range(4):
+            nc.sync.dma_start(out=w8_s[32 * q : 32 * q + 4, :].rearrange("p (g n) -> p g n", g=E), in_=w8_src[q])
+            nc.sync.dma_start(out=w4_s[32 * q : 32 * q + 4, :].rearrange("p (g n) -> p g n", g=2 * E), in_=w4_src[q])
+        EH = E // 2
+        w8 = [keep.tile([P, EH, N], I32, name=f"w8_{h}", align_bytes=64) for h in range(2)]
+        w4 = [keep.tile([P, EH, 2, N // 2], I32, name=f"w4_{h}", align_bytes=64) for h in range(2)]
+        b_sb = keep.tile([P, E], F32, name="b_sb")
+        gate_sb = keep.tile([P, TOP, T], F32, name="gate_sb")
+        for h in range(2):
+            nc.sync.dma_start(
+                out=w8[h][:],
+                in_=w8_words[h * EH : (h + 1) * EH].rearrange("e a p n r -> p (e a) (n r)").bitcast(I32),
+            )
+            nc.sync.dma_start(
+                out=w4[h][:].rearrange("p e a n -> p (e a) n"),
+                in_=w4_words[h * EH : (h + 1) * EH].rearrange("e a p n -> p (e a) n").bitcast(I32),
+            )
+            if h == 0:
+                nc.sync.dma_start(out=b_sb[:], in_=b)
+        for r, pos in enumerate((pos1, pos2, pos3, pos4)):
+            nc.sync.dma_start(pos_sb[r][:], pos)
+        nc.sync.dma_start(out=gate_sb[:], in_=gate.rearrange("r p t -> p r t"))
+
+        xb = [keep.tile([P, T, 4], BF16, name=f"xb{a}", align_bytes=64) for a in range(PASSES)]
+
+        def lay(copy, a, src, c0, c1, s0):
+            copy(
+                out=xb[a][:, c0:c1, :].rearrange("p (c i) j -> p c j i", i=4),
+                in_=src[:, :, c0 - s0 : c1 - s0].rearrange("p j (c i) -> p c j i", i=4),
+            )
+
+        def quantise(a, c0, c1):
+            k = PLANE[a]
+            nc.vector.quantize_mx(
+                out=codes[a][:, c0:c1].bitcast(FP8X4),
+                scales=bytes_all[k:P, c0:c1],
+                in_=xb[a][:, c0:c1, :].rearrange("p n j -> p (n j)"),
+            )
+
+        words = [keep.tile([P, S], U32, name=f"words{a}", align_bytes=64) for a in range(PASSES)]
+        g_bytes = keep.tile([P, S], U8, name="g_bytes", align_bytes=64)
+
+        def gather_words(a, s0, s1):
+            nc.vector.tensor_copy(
+                out=words[a][:, s0:s1], in_=codes[a][:].bitcast(U32).indirect(offs_sb[:, s0 // 16 : s1 // 16])
+            )
+
+        def gather_bytes(s0, s1):
+            nc.vector.tensor_copy(out=g_bytes[:, s0:s1], in_=bytes_all[:].indirect(offs_sb[:, s0 // 16 : s1 // 16]))
+            nc.sync.dma_start(out=g_moved[0 : P - 8, s0 // 4 : s1 // 4], in_=g_bytes[8:P, s0:s1].bitcast(I32))
+
+        lay(nc.vector.tensor_copy, 0, x0a, 0, 384, 0)
+        lay(nc.scalar.copy, 0, x0a, 384, 512, 0)
+        lay(nc.scalar.copy, 0, x0b, 512, 640, 512)
+        quantise(0, 0, 512)
+        quantise(0, 512, 640)
+        for a, src in ((1, x1), (2, x2)):
+            lay(nc.scalar.copy, a, src, 0, 512, 0)
+            lay(nc.scalar.copy, a, src, 512, 640, 0)
+        gather_words(0, 0, HALF)
+        gather_words(0, HALF, S)
+        quantise(1, 0, 512)
+        quantise(1, 512, 640)
+        quantise(2, 0, 512)
+        quantise(2, 512, 640)
+        gather_bytes(0, HALF)
+        gather_bytes(HALF, S)
+
+        y = keep.tile([P, S], F32, name="y")
+        moved8 = g_moved[:].bitcast(U8)
+        w8_s8 = w8_s[:].bitcast(U8)
+        w4_s8 = w4_s[:].bitcast(U8)
+
+        def multiply(e, acc, passes):
+            h, el = divmod(e, EH)
+            cols = slice(e * C, (e + 1) * C)
+            for a in passes:
+                if a == 0:
+                    lhs, lhs_scale, plane = w8[h][:, el, :].bitcast(FP8X4), w8_s8[:, e * N : (e + 1) * N], g_bytes[4:P, cols]
+                else:
+                    g = 2 * e + a - 1
+                    lhs, lhs_scale = w4[h][:, el, a - 1, :].bitcast(FP4X4), w4_s8[:, g * N : (g + 1) * N]
+                    plane = g_bytes[:, cols] if a == 1 else moved8[:, cols]
+                nc.tensor.matmul_mx(
+                    out=acc, lhsT=lhs, lhsT_scale=lhs_scale, rhs=words[a][:, cols].bitcast(FP8X4), rhs_scale=plane,
+                    start=(a == 0), stop=(a == 2),
+                )
+
+        def activate(e, acc):
+            nc.scalar.activation(out=y[:, e * C : (e + 1) * C], in_=acc, func=GELU, bias=b_sb[:, e : e + 1])
+
+        for e0 in range(0, E, 4):
+            ps = psum.tile([P, 512], F32, name="ps")
+            accs = [ps[:, k * C : (k + 1) * C] for k in range(4)]
+            gather_words(1, e0 * C, (e0 + 4) * C)
+            if e0 + 4 < E:
+                gather_words(2, e0 * C, (e0 + 4) * C)
+                for k in range(4):
+                    multiply(e0 + k, accs[k], (0, 1, 2))
+                    activate(e0 + k, accs[k])
+            else:
+                ps_last = psum.tile([P, 512], F32, name="ps")
+                multiply(E - 1, ps_last[:, 0:C], (0, 1))
+                gather_words(2, e0 * C, (E - 1) * C)
+                for k in range(3):
+                    multiply(e0 + k, accs[k], (0, 1, 2))
+                    activate(e0 + k, accs[k])
+                gather_words(2, (E - 1) * C, S)
+                multiply(E - 1, ps_last[:, 0:C], (2,))
+                activate(E - 1, ps_last[:, 0:C])
+
+        prod = [keep.tile([P, T], F32, name=f"prod{r}") for r in range(TOP)]
+        s01 = keep.tile([P, T], F32, name="s01")
+        s23 = keep.tile([P, T], F32, name="s23")
+        res = keep.tile([P, T], F32, name="res")
+
+        def fetch(r):
+            nc.vector.tensor_tensor(prod[r][:], y[:].indirect(pos_sb[r][:]), gate_sb[:, r, :], MULT)
+
+        fetch(0)
+        fetch(1)
+        fetch(2)
+        nc.vector.tensor_tensor(s01[:], prod[0][:], prod[1][:], ADD)
+        fetch(3)
+        TH = T // 2
+        for t0 in (0, TH):
+            cols = slice(t0, t0 + TH)
+            nc.vector.tensor_tensor(s23[:, cols], s01[:, cols], prod[2][:, cols], ADD)
+        for t0 in (0, TH):
+            cols = slice(t0, t0 + TH)
+            nc.vector.tensor_tensor(res[:, cols], s23[:, cols], prod[3][:, cols], ADD)
+            nc.sync.dma_start(out=out[:, cols], in_=res[:, cols])

@@ -33,7 +33,8 @@ def tile_moe_tk_lin_gelu_kernel(
     with ExitStack() as ctx:
         lists = ctx.enter_context(tc.tile_pool(name="lists", bufs=1))
         keep = ctx.enter_context(tc.tile_pool(name="keep", bufs=1))
-        psum = ctx.enter_context(tc.psum_pool(name="psum", bufs=6))
+        late = ctx.enter_context(tc.tile_pool(name="late", bufs=1))
+        psum = ctx.enter_context(tc.psum_pool(name="psum", bufs=8))
 
         offs_sb = lists.tile([P, S // 16], U16, name="offs_sb")
         pos_sb = [lists.tile([P, T // 16], U16, name=f"pos{r}_sb") for r in range(TOP)]
@@ -56,27 +57,22 @@ def tile_moe_tk_lin_gelu_kernel(
         nc.gpsimd.memset(tiny[:], 0.0)
         nc.scalar.activation(out=tiny2[:], in_=tiny[:], func=GELU)
         codes = [keep.tile([P, WIN if a < 1 else WIN2], I32, name=f"codes{a}", align_bytes=64) for a in range(PASSES)]
-        bytes_all = keep.tile([P, WIN], U8, name="bytes_all", align_bytes=64)
+        bytes_all = late.tile([P, WIN], U8, name="bytes_all", tag="late", align_bytes=64)
         nc.gpsimd.memset(bytes_all[:], 0)
         for a in range(PASSES):
             nc.vector.memset(codes[a][:, T:], 0)
-        w8_s = keep.tile([P, E * N // 4], I32, name="w8_s", align_bytes=64)
-        w4_s = keep.tile([P, 2 * E * N // 4], I32, name="w4_s", align_bytes=64)
+        w_s = keep.tile([P, 3 * E * N // 4], I32, name="w_s", align_bytes=64)
         g_moved = keep.tile([P, S // 4], I32, name="g_moved", align_bytes=64)
-        nc.gpsimd.memset(w8_s[:], 0)
-        nc.gpsimd.memset(w4_s[:], 0)
+        nc.gpsimd.memset(w_s[:], 0)
         nc.gpsimd.memset(g_moved[:], 0)
 
-        w8_src = w8_scales.bitcast(I32).rearrange("e a (q r) n -> q r (e a) n", r=4)
-        w4_src = w4_scales.bitcast(I32).rearrange("e a (q r) n -> q r (e a) n", r=4)
-        for q in range(4):
-            nc.sync.dma_start(out=w8_s[32 * q : 32 * q + 4, :].rearrange("p (g n) -> p g n", g=E), in_=w8_src[q])
-            nc.sync.dma_start(out=w4_s[32 * q : 32 * q + 4, :].rearrange("p (g n) -> p g n", g=2 * E), in_=w4_src[q])
+        stage = keep.tile([16, 3 * E, N // 4], I32, name="stage")
+        nc.sync.dma_start(out=stage[:, 0:E, :], in_=w8_scales.bitcast(I32).rearrange("e a q n -> q (e a) n"))
+        nc.sync.dma_start(out=stage[:, E:, :], in_=w4_scales.bitcast(I32).rearrange("e a q n -> q (e a) n"))
         EH = E // 2
         w8 = [keep.tile([P, EH, N], I32, name=f"w8_{h}", align_bytes=64) for h in range(2)]
         w4 = [keep.tile([P, EH, 2, N // 2], I32, name=f"w4_{h}", align_bytes=64) for h in range(2)]
         b_sb = keep.tile([P, E], F32, name="b_sb")
-        gate_sb = keep.tile([P, TOP, T], F32, name="gate_sb")
         for h in range(2):
             nc.sync.dma_start(
                 out=w8[h][:],
@@ -87,10 +83,14 @@ def tile_moe_tk_lin_gelu_kernel(
                 in_=w4_words[h * EH : (h + 1) * EH].rearrange("e a p n -> p (e a) n").bitcast(I32),
             )
             if h == 0:
+                for q in range(4):
+                    nc.sync.dma_start(
+                        out=w_s[32 * q : 32 * q + 4, :],
+                        in_=stage[4 * q : 4 * q + 4, :, :].rearrange("p g n -> p (g n)"),
+                    )
                 nc.sync.dma_start(out=b_sb[:], in_=b)
         for r, pos in enumerate((pos1, pos2, pos3, pos4)):
             nc.sync.dma_start(pos_sb[r][:], pos)
-        nc.sync.dma_start(out=gate_sb[:], in_=gate.rearrange("r p t -> p r t"))
 
         xb = [keep.tile([P, T, 4], BF16, name=f"xb{a}", align_bytes=64) for a in range(PASSES)]
 
@@ -125,32 +125,29 @@ def tile_moe_tk_lin_gelu_kernel(
         lay(nc.scalar.copy, 0, x0b, 512, 640, 512)
         quantise(0, 0, 512)
         quantise(0, 512, 640)
-        for a, src in ((1, x1), (2, x2)):
-            lay(nc.scalar.copy, a, src, 0, 512, 0)
-            lay(nc.scalar.copy, a, src, 512, 640, 0)
+        lay(nc.scalar.copy, 1, x1, 0, 640, 0)
+        lay(nc.scalar.copy, 2, x2, 0, 384, 0)
         gather_words(0, 0, HALF)
         gather_words(0, HALF, S)
-        quantise(1, 0, 512)
-        quantise(1, 512, 640)
+        lay(nc.vector.tensor_copy, 2, x2, 384, 640, 0)
         quantise(2, 0, 512)
         quantise(2, 512, 640)
-        gather_bytes(0, HALF)
-        gather_bytes(HALF, S)
+        quantise(1, 0, 512)
+        quantise(1, 512, 640)
 
         y = keep.tile([P, S], F32, name="y")
         moved8 = g_moved[:].bitcast(U8)
-        w8_s8 = w8_s[:].bitcast(U8)
-        w4_s8 = w4_s[:].bitcast(U8)
+        w_s8 = w_s[:].bitcast(U8)
 
         def multiply(e, acc, passes):
             h, el = divmod(e, EH)
             cols = slice(e * C, (e + 1) * C)
             for a in passes:
                 if a == 0:
-                    lhs, lhs_scale, plane = w8[h][:, el, :].bitcast(FP8X4), w8_s8[:, e * N : (e + 1) * N], g_bytes[4:P, cols]
+                    lhs, lhs_scale, plane = w8[h][:, el, :].bitcast(FP8X4), w_s8[:, e * N : (e + 1) * N], g_bytes[4:P, cols]
                 else:
-                    g = 2 * e + a - 1
-                    lhs, lhs_scale = w4[h][:, el, a - 1, :].bitcast(FP4X4), w4_s8[:, g * N : (g + 1) * N]
+                    g = E + 2 * e + a - 1
+                    lhs, lhs_scale = w4[h][:, el, a - 1, :].bitcast(FP4X4), w_s8[:, g * N : (g + 1) * N]
                     plane = g_bytes[:, cols] if a == 1 else moved8[:, cols]
                 nc.tensor.matmul_mx(
                     out=acc, lhsT=lhs, lhsT_scale=lhs_scale, rhs=words[a][:, cols].bitcast(FP8X4), rhs_scale=plane,
@@ -160,25 +157,21 @@ def tile_moe_tk_lin_gelu_kernel(
         def activate(e, acc):
             nc.scalar.activation(out=y[:, e * C : (e + 1) * C], in_=acc, func=GELU, bias=b_sb[:, e : e + 1])
 
+        gather_bytes(0, HALF)
+        gather_bytes(HALF, S)
+        gate_sb = late.tile([P, TOP, T], F32, name="gate_sb", tag="late", align_bytes=64)
+        nc.sync.dma_start(out=gate_sb[:], in_=gate.rearrange("r p t -> p r t"))
+        accs = {}
         for e0 in range(0, E, 4):
-            ps = psum.tile([P, 512], F32, name="ps")
-            accs = [ps[:, k * C : (k + 1) * C] for k in range(4)]
             gather_words(1, e0 * C, (e0 + 4) * C)
-            if e0 + 4 < E:
-                gather_words(2, e0 * C, (e0 + 4) * C)
-                for k in range(4):
-                    multiply(e0 + k, accs[k], (0, 1, 2))
-                    activate(e0 + k, accs[k])
-            else:
-                ps_last = psum.tile([P, 512], F32, name="ps")
-                multiply(E - 1, ps_last[:, 0:C], (0, 1))
-                gather_words(2, e0 * C, (E - 1) * C)
-                for k in range(3):
-                    multiply(e0 + k, accs[k], (0, 1, 2))
-                    activate(e0 + k, accs[k])
-                gather_words(2, (E - 1) * C, S)
-                multiply(E - 1, ps_last[:, 0:C], (2,))
-                activate(E - 1, ps_last[:, 0:C])
+            for e in range(e0, e0 + 4):
+                accs[e] = psum.tile([P, C], F32, name="acc")
+                multiply(e, accs[e][:], (0, 1))
+            for a, z in ((e0, e0 + 4),) if e0 + 4 < E else ((e0, E - 1), (E - 1, E)):
+                gather_words(2, a * C, z * C)
+                for e in range(a, z):
+                    multiply(e, accs[e][:], (2,))
+                    activate(e, accs[e][:])
 
         prod = [keep.tile([P, T], F32, name=f"prod{r}") for r in range(TOP)]
         s01 = keep.tile([P, T], F32, name="s01")

@@ -57,8 +57,9 @@ def tile_moe_tk_lin_gelu_kernel(
         nc.gpsimd.memset(tiny[:], 0.0)
         nc.scalar.activation(out=tiny2[:], in_=tiny[:], func=GELU)
         codes = [keep.tile([P, WIN if a < 1 else WIN2], I32, name=f"codes{a}", align_bytes=64) for a in range(PASSES)]
-        bytes_all = late.tile([P, WIN], U8, name="bytes_all", tag="late", align_bytes=64)
-        nc.gpsimd.memset(bytes_all[:], 0)
+        bytes_i32 = late.tile([P, WIN // 4], I32, name="bytes_i32", tag="late", align_bytes=64)
+        bytes_all = bytes_i32[:].bitcast(U8)
+        nc.vector.memset(bytes_i32[:], 0)
         for a in range(PASSES):
             nc.vector.memset(codes[a][:, T:], 0)
         w_s = keep.tile([P, 3 * E * N // 4], I32, name="w_s", align_bytes=64)
@@ -73,22 +74,28 @@ def tile_moe_tk_lin_gelu_kernel(
         w8 = [keep.tile([P, EH, N], I32, name=f"w8_{h}", align_bytes=64) for h in range(2)]
         w4 = [keep.tile([P, EH, 2, N // 2], I32, name=f"w4_{h}", align_bytes=64) for h in range(2)]
         b_sb = keep.tile([P, E], F32, name="b_sb")
-        for h in range(2):
+
+        def load_w8(h):
             nc.sync.dma_start(
                 out=w8[h][:],
                 in_=w8_words[h * EH : (h + 1) * EH].rearrange("e a p n r -> p (e a) (n r)").bitcast(I32),
             )
+
+        def load_w4(h):
             nc.sync.dma_start(
                 out=w4[h][:].rearrange("p e a n -> p (e a) n"),
                 in_=w4_words[h * EH : (h + 1) * EH].rearrange("e a p n -> p (e a) n").bitcast(I32),
             )
-            if h == 0:
-                for q in range(4):
-                    nc.sync.dma_start(
-                        out=w_s[32 * q : 32 * q + 4, :],
-                        in_=stage[4 * q : 4 * q + 4, :, :].rearrange("p g n -> p (g n)"),
-                    )
-                nc.sync.dma_start(out=b_sb[:], in_=b)
+
+        load_w8(0)
+        for q in range(4):
+            nc.sync.dma_start(
+                out=w_s[32 * q : 32 * q + 4, :], in_=stage[4 * q : 4 * q + 4, :, :].rearrange("p g n -> p (g n)")
+            )
+        load_w4(0)
+        nc.sync.dma_start(out=b_sb[:], in_=b)
+        load_w8(1)
+        load_w4(1)
         for r, pos in enumerate((pos1, pos2, pos3, pos4)):
             nc.sync.dma_start(pos_sb[r][:], pos)
 
@@ -117,7 +124,7 @@ def tile_moe_tk_lin_gelu_kernel(
             )
 
         def gather_bytes(s0, s1):
-            nc.vector.tensor_copy(out=g_bytes[:, s0:s1], in_=bytes_all[:].indirect(offs_sb[:, s0 // 16 : s1 // 16]))
+            nc.vector.tensor_copy(out=g_bytes[:, s0:s1], in_=bytes_all.indirect(offs_sb[:, s0 // 16 : s1 // 16]))
             nc.sync.dma_start(out=g_moved[0 : P - 8, s0 // 4 : s1 // 4], in_=g_bytes[8:P, s0:s1].bitcast(I32))
 
         lay(nc.vector.tensor_copy, 0, x0a, 0, 384, 0)
@@ -157,21 +164,35 @@ def tile_moe_tk_lin_gelu_kernel(
         def activate(e, acc):
             nc.scalar.activation(out=y[:, e * C : (e + 1) * C], in_=acc, func=GELU, bias=b_sb[:, e : e + 1])
 
-        gather_bytes(0, HALF)
-        gather_bytes(HALF, S)
-        gate_sb = late.tile([P, TOP, T], F32, name="gate_sb", tag="late", align_bytes=64)
-        nc.sync.dma_start(out=gate_sb[:], in_=gate.rearrange("r p t -> p r t"))
         accs = {}
-        for e0 in range(0, E, 4):
+
+        def first_two(e0):
             gather_words(1, e0 * C, (e0 + 4) * C)
             for e in range(e0, e0 + 4):
                 accs[e] = psum.tile([P, C], F32, name="acc")
                 multiply(e, accs[e][:], (0, 1))
-            for a, z in ((e0, e0 + 4),) if e0 + 4 < E else ((e0, E - 1), (E - 1, E)):
-                gather_words(2, a * C, z * C)
-                for e in range(a, z):
-                    multiply(e, accs[e][:], (2,))
-                    activate(e, accs[e][:])
+
+        def third(e0, e1):
+            gather_words(2, e0 * C, e1 * C)
+            for e in range(e0, e1):
+                multiply(e, accs[e][:], (2,))
+                activate(e, accs[e][:])
+
+        gather_bytes(0, HALF)
+        first_two(0)
+        first_two(4)
+        gather_bytes(HALF, S)
+        gate_sb = late.tile([P, TOP, T], F32, name="gate_sb", tag="late", align_bytes=64)
+        nc.sync.dma_start(out=gate_sb[:], in_=gate.rearrange("r p t -> p r t"))
+        third(0, 4)
+        third(4, 8)
+        first_two(8)
+        third(8, 12)
+        first_two(12)
+        third(12, 16)
+        first_two(16)
+        third(16, 19)
+        third(19, 20)
 
         prod = [keep.tile([P, T], F32, name=f"prod{r}") for r in range(TOP)]
         s01 = keep.tile([P, T], F32, name="s01")

@@ -34,6 +34,7 @@ def tile_moe_tk_lin_gelu_kernel(
         lists = ctx.enter_context(tc.tile_pool(name="lists", bufs=1))
         keep = ctx.enter_context(tc.tile_pool(name="keep", bufs=1))
         late = ctx.enter_context(tc.tile_pool(name="late", bufs=1))
+        hold = ctx.enter_context(tc.tile_pool(name="hold", bufs=1))
         psum = ctx.enter_context(tc.psum_pool(name="psum", bufs=8))
 
         offs_sb = lists.tile([P, S // 16], U16, name="offs_sb")
@@ -99,7 +100,8 @@ def tile_moe_tk_lin_gelu_kernel(
         for r, pos in enumerate((pos1, pos2, pos3, pos4)):
             nc.sync.dma_start(pos_sb[r][:], pos)
 
-        xb = [keep.tile([P, T, 4], BF16, name=f"xb{a}", align_bytes=64) for a in range(PASSES)]
+        xb = [keep.tile([P, T, 4], BF16, name=f"xb{a}", align_bytes=64) for a in range(2)]
+        xb.append(hold.tile([P, T, 4], BF16, name="xb2", tag="hold", align_bytes=64))
 
         def lay(copy, a, src, c0, c1, s0):
             copy(
@@ -115,17 +117,23 @@ def tile_moe_tk_lin_gelu_kernel(
                 in_=xb[a][:, c0:c1, :].rearrange("p n j -> p (n j)"),
             )
 
-        words = [keep.tile([P, S], U32, name=f"words{a}", align_bytes=64) for a in range(PASSES)]
+        words = {(a, 0): keep.tile([P, S], U32, name=f"words{a}", align_bytes=64) for a in (0, 2)}
+        words[1, 0] = keep.tile([P, 8 * C], U32, name="words1a", align_bytes=64)
         g_bytes = keep.tile([P, S], U8, name="g_bytes", align_bytes=64)
+
+        def word_cols(a, s0, s1):
+            if a == 1 and s0 >= 8 * C:
+                return words[1, 1][:, s0 - 8 * C : s1 - 8 * C]
+            return words[a, 0][:, s0:s1]
 
         def gather_words(a, s0, s1):
             nc.vector.tensor_copy(
-                out=words[a][:, s0:s1], in_=codes[a][:].bitcast(U32).indirect(offs_sb[:, s0 // 16 : s1 // 16])
+                out=word_cols(a, s0, s1), in_=codes[a][:].bitcast(U32).indirect(offs_sb[:, s0 // 16 : s1 // 16])
             )
 
         def gather_bytes(s0, s1):
             nc.vector.tensor_copy(out=g_bytes[:, s0:s1], in_=bytes_all.indirect(offs_sb[:, s0 // 16 : s1 // 16]))
-            nc.sync.dma_start(out=g_moved[0 : P - 8, s0 // 4 : s1 // 4], in_=g_bytes[8:P, s0:s1].bitcast(I32))
+            nc.scalar.dma_start(out=g_moved[0 : P - 8, s0 // 4 : s1 // 4], in_=g_bytes[8:P, s0:s1].bitcast(I32))
 
         lay(nc.vector.tensor_copy, 0, x0a, 0, 384, 0)
         lay(nc.scalar.copy, 0, x0a, 384, 512, 0)
@@ -133,14 +141,16 @@ def tile_moe_tk_lin_gelu_kernel(
         quantise(0, 0, 512)
         quantise(0, 512, 640)
         lay(nc.scalar.copy, 1, x1, 0, 640, 0)
-        lay(nc.scalar.copy, 2, x2, 0, 384, 0)
+        lay(nc.scalar.copy, 2, x2, 0, 640, 0)
         gather_words(0, 0, HALF)
         gather_words(0, HALF, S)
-        lay(nc.vector.tensor_copy, 2, x2, 384, 640, 0)
-        quantise(2, 0, 512)
-        quantise(2, 512, 640)
         quantise(1, 0, 512)
         quantise(1, 512, 640)
+        gather_words(1, 0, 4 * C)
+        gather_words(1, 4 * C, 8 * C)
+        quantise(2, 0, 512)
+        quantise(2, 512, 640)
+        words[1, 1] = hold.tile([P, S - 8 * C], U32, name="words1b", tag="hold", align_bytes=64)
 
         y = keep.tile([P, S], F32, name="y")
         moved8 = g_moved[:].bitcast(U8)
@@ -157,7 +167,7 @@ def tile_moe_tk_lin_gelu_kernel(
                     lhs, lhs_scale = w4[h][:, el, a - 1, :].bitcast(FP4X4), w_s8[:, g * N : (g + 1) * N]
                     plane = g_bytes[:, cols] if a == 1 else moved8[:, cols]
                 nc.tensor.matmul_mx(
-                    out=acc, lhsT=lhs, lhsT_scale=lhs_scale, rhs=words[a][:, cols].bitcast(FP8X4), rhs_scale=plane,
+                    out=acc, lhsT=lhs, lhsT_scale=lhs_scale, rhs=word_cols(a, e * C, (e + 1) * C).bitcast(FP8X4), rhs_scale=plane,
                     start=(a == 0), stop=(a == 2),
                 )
 
@@ -167,7 +177,8 @@ def tile_moe_tk_lin_gelu_kernel(
         accs = {}
 
         def first_two(e0):
-            gather_words(1, e0 * C, (e0 + 4) * C)
+            if e0 >= 8:
+                gather_words(1, e0 * C, (e0 + 4) * C)
             for e in range(e0, e0 + 4):
                 accs[e] = psum.tile([P, C], F32, name="acc")
                 multiply(e, accs[e][:], (0, 1))

from contextlib import ExitStack

import concourse.mybir as mybir

F32 = mybir.dt.float32
BF16 = mybir.dt.bfloat16
I32 = mybir.dt.int32
U32 = mybir.dt.uint32
U16 = mybir.dt.uint16
U8 = mybir.dt.uint8
FP8X4 = mybir.dt.float8_e4m3fn_x4
FP4X4 = mybir.dt.float4_e2m1fn_x4
MULT = mybir.AluOpType.mult
ADD = mybir.AluOpType.add
GELU = mybir.ActivationFunctionType.Gelu_apprx_tanh

P = 128
K, T, E, C, N, TOP = 1536, 640, 20, 128, 128, 4
PASSES = 3
S = E * C
FLOPS = 2 * S * K * N

WIN = 1728
HALF = S // 2
WIN2 = 704
PLANE = (4, 0, 8)


def tile_moe_tk_lin_gelu_kernel(
    tc, xT, w8_words, w8_scales, w4_words, w4_scales, b, gate, offs, pos1, pos2, pos3, pos4, out
):
    nc = tc.nc
    with ExitStack() as ctx:
        lists = ctx.enter_context(tc.tile_pool(name="lists", bufs=1))
        keep = ctx.enter_context(tc.tile_pool(name="keep", bufs=1))
        late = ctx.enter_context(tc.tile_pool(name="late", bufs=1))
        hold = ctx.enter_context(tc.tile_pool(name="hold", bufs=1))
        psum = ctx.enter_context(tc.psum_pool(name="psum", bufs=8))

        offs_sb = lists.tile([P, S // 16], U16, name="offs_sb")
        pos_sb = [lists.tile([P, T // 16], U16, name=f"pos{r}_sb") for r in range(TOP)]

        def x_rows(a):
            return xT[512 * a : 512 * (a + 1), :].rearrange("(p j) t -> p j t", j=4)

        x0a = keep.tile([P, 4, 512], F32, name="x0a")
        x0b = keep.tile([P, 4, 128], F32, name="x0b")
        x1 = keep.tile([P, 4, T], F32, name="x1")
        x2 = keep.tile([P, 4, T], F32, name="x2")
        nc.sync.dma_start(out=x0a[:], in_=x_rows(0)[:, :, 0:512])
        nc.sync.dma_start(out=x0b[:], in_=x_rows(0)[:, :, 512:640])
        nc.sync.dma_start(offs_sb[:], offs)
        nc.sync.dma_start(out=x1[:], in_=x_rows(1))
        nc.sync.dma_start(out=x2[:], in_=x_rows(2))

        tiny = keep.tile([P, 8], F32, name="tiny")
        tiny2 = keep.tile([P, 8], F32, name="tiny2")
        nc.gpsimd.memset(tiny[:], 0.0)
        nc.scalar.activation(out=tiny2[:], in_=tiny[:], func=GELU)
        codes = [keep.tile([P, WIN if a < 1 else WIN2], I32, name=f"codes{a}", align_bytes=64) for a in range(PASSES)]
        bytes_i32 = late.tile([P, WIN // 4], I32, name="bytes_i32", tag="late", align_bytes=64)
        bytes_all = bytes_i32[:].bitcast(U8)
        nc.vector.memset(bytes_i32[:], 0)
        for a in range(PASSES):
            nc.vector.memset(codes[a][:, T:], 0)
        w_s = keep.tile([P, 3 * E * N // 4], I32, name="w_s", align_bytes=64)
        g_moved = keep.tile([P, S // 4], I32, name="g_moved", align_bytes=64)
        nc.gpsimd.memset(w_s[:], 0)
        nc.gpsimd.memset(g_moved[:], 0)

        stage = keep.tile([16, 3 * E, N // 4], I32, name="stage")
        nc.sync.dma_start(out=stage[:, 0:E, :], in_=w8_scales.bitcast(I32).rearrange("e a q n -> q (e a) n"))
        nc.sync.dma_start(out=stage[:, E:, :], in_=w4_scales.bitcast(I32).rearrange("e a q n -> q (e a) n"))
        EH = E // 2
        w8 = [keep.tile([P, EH, N], I32, name=f"w8_{h}", align_bytes=64) for h in range(2)]
        w4 = [keep.tile([P, EH, 2, N // 2], I32, name=f"w4_{h}", align_bytes=64) for h in range(2)]
        b_sb = keep.tile([P, E], F32, name="b_sb")

        def load_w8(h):
            nc.sync.dma_start(
                out=w8[h][:],
                in_=w8_words[h * EH : (h + 1) * EH].rearrange("e a p n r -> p (e a) (n r)").bitcast(I32),
            )

        def load_w4(h):
            nc.sync.dma_start(
                out=w4[h][:].rearrange("p e a n -> p (e a) n"),
                in_=w4_words[h * EH : (h + 1) * EH].rearrange("e a p n -> p (e a) n").bitcast(I32),
            )

        load_w8(0)
        for q in range(4):
            nc.sync.dma_start(
                out=w_s[32 * q : 32 * q + 4, :], in_=stage[4 * q : 4 * q + 4, :, :].rearrange("p g n -> p (g n)")
            )
        load_w4(0)
        nc.sync.dma_start(out=b_sb[:], in_=b)
        load_w8(1)
        load_w4(1)
        for r, pos in enumerate((pos1, pos2, pos3, pos4)):
            nc.sync.dma_start(pos_sb[r][:], pos)

        xb = [keep.tile([P, T, 4], BF16, name=f"xb{a}", align_bytes=64) for a in range(2)]
        xb.append(hold.tile([P, T, 4], BF16, name="xb2", tag="hold", align_bytes=64))

        def lay(copy, a, src, c0, c1, s0):
            copy(
                out=xb[a][:, c0:c1, :].rearrange("p (c i) j -> p c j i", i=4),
                in_=src[:, :, c0 - s0 : c1 - s0].rearrange("p j (c i) -> p c j i", i=4),
            )

        def quantise(a, c0, c1):
            k = PLANE[a]
            nc.vector.quantize_mx(
                out=codes[a][:, c0:c1].bitcast(FP8X4),
                scales=bytes_all[k:P, c0:c1],
                in_=xb[a][:, c0:c1, :].rearrange("p n j -> p (n j)"),
            )

        words = {(a, 0): keep.tile([P, S], U32, name=f"words{a}", align_bytes=64) for a in (0, 2)}
        words[1, 0] = keep.tile([P, 8 * C], U32, name="words1a", align_bytes=64)
        g_bytes = keep.tile([P, S], U8, name="g_bytes", align_bytes=64)

        def word_cols(a, s0, s1):
            if a == 1 and s0 >= 8 * C:
                return words[1, 1][:, s0 - 8 * C : s1 - 8 * C]
            return words[a, 0][:, s0:s1]

        def gather_words(a, s0, s1):
            nc.vector.tensor_copy(
                out=word_cols(a, s0, s1), in_=codes[a][:].bitcast(U32).indirect(offs_sb[:, s0 // 16 : s1 // 16])
            )

        def gather_bytes(s0, s1):
            nc.vector.tensor_copy(out=g_bytes[:, s0:s1], in_=bytes_all.indirect(offs_sb[:, s0 // 16 : s1 // 16]))
            nc.scalar.dma_start(out=g_moved[0 : P - 8, s0 // 4 : s1 // 4], in_=g_bytes[8:P, s0:s1].bitcast(I32))

        lay(nc.vector.tensor_copy, 0, x0a, 0, 384, 0)
        lay(nc.scalar.copy, 0, x0a, 384, 512, 0)
        lay(nc.scalar.copy, 0, x0b, 512, 640, 512)
        quantise(0, 0, 512)
        quantise(0, 512, 640)
        lay(nc.scalar.copy, 1, x1, 0, 640, 0)
        lay(nc.scalar.copy, 2, x2, 0, 640, 0)
        gather_words(0, 0, HALF)
        gather_words(0, HALF, S)
        quantise(1, 0, 512)
        quantise(1, 512, 640)
        gather_words(1, 0, 4 * C)
        gather_words(1, 4 * C, 8 * C)
        quantise(2, 0, 512)
        quantise(2, 512, 640)
        words[1, 1] = hold.tile([P, S - 8 * C], U32, name="words1b", tag="hold", align_bytes=64)

        y = keep.tile([P, S], F32, name="y")
        moved8 = g_moved[:].bitcast(U8)
        w_s8 = w_s[:].bitcast(U8)

        def multiply(e, acc, passes):
            h, el = divmod(e, EH)
            cols = slice(e * C, (e + 1) * C)
            for a in passes:
                if a == 0:
                    lhs, lhs_scale, plane = w8[h][:, el, :].bitcast(FP8X4), w_s8[:, e * N : (e + 1) * N], g_bytes[4:P, cols]
                else:
                    g = E + 2 * e + a - 1
                    lhs, lhs_scale = w4[h][:, el, a - 1, :].bitcast(FP4X4), w_s8[:, g * N : (g + 1) * N]
                    plane = g_bytes[:, cols] if a == 1 else moved8[:, cols]
                nc.tensor.matmul_mx(
                    out=acc, lhsT=lhs, lhsT_scale=lhs_scale, rhs=word_cols(a, e * C, (e + 1) * C).bitcast(FP8X4), rhs_scale=plane,
                    start=(a == 0), stop=(a == 2),
                )

        def activate(e, acc):
            nc.scalar.activation(out=y[:, e * C : (e + 1) * C], in_=acc, func=GELU, bias=b_sb[:, e : e + 1])

        accs = {}

        def first_two(e0):
            if e0 >= 8:
                gather_words(1, e0 * C, (e0 + 4) * C)
            for e in range(e0, e0 + 4):
                accs[e] = psum.tile([P, C], F32, name="acc")
                multiply(e, accs[e][:], (0, 1))

        def third(e0, e1):
            gather_words(2, e0 * C, e1 * C)
            for e in range(e0, e1):
                multiply(e, accs[e][:], (2,))
                activate(e, accs[e][:])

        gather_bytes(0, HALF)
        first_two(0)
        first_two(4)
        gather_bytes(HALF, S)
        gate_sb = late.tile([P, TOP, T], F32, name="gate_sb", tag="late", align_bytes=64)
        nc.sync.dma_start(out=gate_sb[:], in_=gate.rearrange("r p t -> p r t"))
        third(0, 4)
        third(4, 8)
        first_two(8)
        third(8, 12)
        first_two(12)
        third(12, 16)
        first_two(16)
        third(16, 19)
        third(19, 20)

        prod = [keep.tile([P, T], F32, name=f"prod{r}") for r in range(TOP)]
        s01 = keep.tile([P, T], F32, name="s01")
        s23 = keep.tile([P, T], F32, name="s23")
        res = keep.tile([P, T], F32, name="res")

        def fetch(r):
            nc.vector.tensor_tensor(prod[r][:], y[:].indirect(pos_sb[r][:]), gate_sb[:, r, :], MULT)

        fetch(0)
        fetch(1)
        fetch(2)
        nc.vector.tensor_tensor(s01[:], prod[0][:], prod[1][:], ADD)
        fetch(3)
        TH = T // 2
        for t0 in (0, TH):
            cols = slice(t0, t0 + TH)
            nc.vector.tensor_tensor(s23[:, cols], s01[:, cols], prod[2][:, cols], ADD)
        for t0 in (0, TH):
            cols = slice(t0, t0 + TH)
            nc.vector.tensor_tensor(res[:, cols], s23[:, cols], prod[3][:, cols], ADD)
            nc.sync.dma_start(out=out[:, cols], in_=res[:, cols])
